import numpy as np
import ml_dtypes


def mxq(x, axis, fmt="e4m3"):
    dtype, down = {"e4m3": (ml_dtypes.float8_e4m3fn, 7), "e5m2": (ml_dtypes.float8_e5m2, 14)}[fmt]
    v = np.moveaxis(np.asarray(x, np.float32).astype(ml_dtypes.bfloat16).astype(np.float64), axis, -1)
    blocks = v.reshape(v.shape[:-1] + (-1, 32))
    amax = np.abs(blocks).max(-1, keepdims=True)
    byte = np.maximum(np.where(amax > 0, np.frexp(amax)[1] - 1 + 127, 0) - down, 1)
    scale = np.exp2(byte - 127.0)
    codes = (blocks / scale).astype(np.float32).astype(dtype).astype(np.float64)
    return np.moveaxis((codes * scale).reshape(v.shape), -1, axis)


WIDE = False


def mx_kscale(k):
    if not WIDE:
        return np.ones(k)
    levels = np.array([10, -10, 5, -5, 0])
    if k % 512:
        return np.exp2(np.random.permutation(np.resize(levels, k // 32))).repeat(32)
    a = np.empty((k // 512, 16))
    for p in range(k // 512):
        a[p, :8] = np.random.permutation(np.resize(levels, 8))
        for g in range(8):
            far = levels[np.abs(levels - a[p, g]) >= 10]
            a[p, g + 8] = far[np.random.randint(len(far))]
    return np.exp2(a.ravel()).repeat(32)


def f64(x):
    return np.asarray(x).astype(np.float64)


def striped(idx):
    return np.tile(np.asarray(idx).reshape(-1, 16).T, (8, 1)).astype(np.uint16)


def unstriped(offs):
    return offs[:16].T.reshape(-1).astype(np.int64)


E2M1 = np.array([0.0, 0.5, 1.0, 1.5, 2.0, 3.0, 4.0, 6.0, -0.0, -0.5, -1.0, -1.5, -2.0, -3.0, -4.0, -6.0])


def pack_weight(w, fmt):
    k, n = w.shape
    w = f64(np.asarray(w, np.float32).astype(ml_dtypes.bfloat16)).reshape(k // 32, 32, n)
    amax = np.abs(w).max(1)
    if fmt == "e4m3":
        byte = np.frexp(amax)[1] - 1 + 127 - 7
    else:
        mant, ex = np.frexp(amax / 6.0)
        byte = np.where(mant > 0.5, ex, ex - 1) + 127
    byte = np.clip(np.where(amax > 0, byte, 1), 1, 254)
    scaled = (w * np.exp2(127.0 - byte)[:, None, :]).reshape(k, n).astype(np.float32)
    by_word = np.ascontiguousarray(scaled.reshape(k // 512, 128, 4, n).transpose(0, 1, 3, 2))
    if fmt == "e4m3":
        words = by_word.astype(ml_dtypes.float8_e4m3fn).view(np.uint8)
    else:
        c = by_word.astype(ml_dtypes.float4_e2m1fn).view(np.uint8) & 0xF
        words = (c[..., 0::2] | (c[..., 1::2] << 4)).reshape(k // 512, 128, 2 * n)
    return np.ascontiguousarray(words), np.ascontiguousarray(byte.astype(np.uint8).reshape(k // 512, 16, n))


def unpack_weight(words, scales, fmt):
    g, _, n = scales.shape
    words = np.ascontiguousarray(words).reshape(g, 128, n, -1)
    if fmt == "e4m3":
        vals = words.view(ml_dtypes.float8_e4m3fn).astype(np.float64)
    else:
        nib = np.empty((g, 128, n, 4), np.uint8)
        nib[..., 0::2] = words & 0xF
        nib[..., 1::2] = words >> 4
        vals = E2M1[nib]
    vals = vals * np.repeat(np.exp2(scales.astype(np.float64) - 127.0), 8, axis=1)[..., None]
    return vals.transpose(0, 1, 3, 2).reshape(g * 512, n)


def bf(x):
    return np.asarray(x, np.float32).astype(ml_dtypes.bfloat16)


def planes(Y):
    r, m = Y.shape
    b = f64(bf(Y)).reshape(r // 32, 32, m)
    amax = np.abs(b).max(1)
    byte = np.clip(np.where(amax > 0, np.frexp(amax)[1] - 1 + 127 - 7, 1), 1, 254)
    codes = (b * np.exp2(127.0 - byte)[:, None, :]).reshape(r, m).astype(np.float32).astype(ml_dtypes.float8_e4m3fn).view(np.uint8)
    words = codes.reshape(r // 512, 128, 4, m).transpose(0, 1, 3, 2)
    return np.ascontiguousarray(words), np.ascontiguousarray(byte.astype(np.uint8).reshape(r // 512, 16, m))


D, T, I, J, U, E, M = 512, 2048, 512, 256, 1024, 512, 1024


def setup_inputs():
    n = np.random.standard_normal
    idx = np.random.permutation(T)[:I]
    idx2 = np.random.permutation(U)[:J]
    idx3 = np.random.permutation(U)[:J]
    idx4 = np.random.permutation(M)[:J]
    fd = mx_kscale(D)
    fi = mx_kscale(I)
    ti = np.ones(T)
    ti[idx] = fi
    keysp = pack_weight(n((D, T)) / fd[:, None], "e2m1")
    return {
        "keys_words": keysp[0],
        "keys_scales": keysp[1],
        "notes": (n((D, U)) * 1.0 / np.sqrt(D) * fd[:, None]).astype(np.float32),
        "rowf": (np.random.uniform(0.02, 0.08, (I, 1)) * fi[:, None]).astype(np.float32),
        "vals": (n((E, T)) / ti).astype(np.float32),
        "held": (n((E, M))).astype(np.float32),
        "hgain": np.tile(np.random.uniform(0.5, 2.0, M), (128, 1)).astype(np.float32),
        "offs": striped(idx),
        "offs2": striped(idx2),
        "offs3": striped(idx3),
        "offs4": striped(idx4),
    }


def reference(keys_words, keys_scales, notes, rowf, vals, held, hgain, offs, offs2, offs3, offs4):
    idx = unstriped(offs)
    idx2 = unstriped(offs2)
    idx3 = unstriped(offs3)
    idx4 = unstriped(offs4)
    keysu = unpack_weight(keys_words, keys_scales, "e2m1")
    keysidxg = keysu[:, idx]
    notesq = mxq(f64(notes), 0, "e4m3")
    g1 = keysidxg.T @ notesq
    g9 = g1[:, idx2] - g1[:, idx3]
    g0 = np.maximum(g9, 0.0)
    gr1 = g0 * f64(rowf)
    vt1 = f64(vals)[:, idx].T
    vt1q = mxq(vt1, 0, "e4m3")
    gr1q = mxq(gr1, 0, "e4m3")
    o = vt1q.T @ gr1q
    y = f64(held)[:, idx4] + o * f64(hgain)[:1][:, idx4]
    words, scales = planes(y)
    return y, words, scales

@@ -1,0 +1,268 @@
+from contextlib import ExitStack
+
+import concourse.mybir as mybir
+from concourse.masks import make_identity
+
+D, T, I, J, U, E, M = 512, 2048, 512, 256, 1024, 512, 1024
+FLOPS = 2 * D * I * U + 2 * I * E * J
+BYTES = 9631744
+
+F32 = mybir.dt.float32
+BF16 = mybir.dt.bfloat16
+I32 = mybir.dt.int32
+U32 = mybir.dt.uint32
+U16 = mybir.dt.uint16
+U8 = mybir.dt.uint8
+FP8X4 = mybir.dt.float8_e4m3fn_x4
+FP4X4 = mybir.dt.float4_e2m1fn_x4
+ALU = mybir.AluOpType
+COPY = mybir.ActivationFunctionType.Copy
+
+P = 128
+PACK = 4
+BANK = 512
+Y_SHARE = 80
+NOTE_CHUNKS = ((0, 512, 256), (512, 256, 256), (768, 256, 128))
+
+
+def interleave(copy, dst, src):
+    copy(out=dst.rearrange("p (c i) t -> p c t i", i=4), in_=src.rearrange("p t (c i) -> p c t i", i=4))
+
+
+def tile_attend_tab_looked_merge_pl_kernel(
+    tc, keys_words, keys_scales, notes, rowf, vals, held, hgain, offs, offs2, offs3, offs4, out_0, out_1, out_2
+):
+    nc = tc.nc
+    with ExitStack() as ctx:
+        lists = ctx.enter_context(tc.tile_pool(name="lists", bufs=1))
+        sb = ctx.enter_context(tc.tile_pool(name="sb", bufs=1))
+        ps = ctx.enter_context(tc.psum_pool(name="ps", bufs=1))
+
+        def bank(n, shape, name):
+            return ps.tile(shape, F32, name=name, tag=f"bank{n}")
+
+        def tiles(name, count, shape, dtype):
+            return [sb.tile(shape, dtype, name=f"{name}{n}", align_bytes=64) for n in range(count)]
+
+        idx = lists.tile([P, I // 16], U16)
+        idx2 = lists.tile([P, J // 16], U16)
+        idx3 = lists.tile([P, J // 16], U16)
+        idx4 = lists.tile([P, J // 16], U16)
+        key_pool = sb.tile([P, T], U16, align_bytes=64)
+        key_scale_pool = sb.tile([P, T], U8, align_bytes=64)
+        gain_cols = sb.tile([P, M // P], F32)
+        row_factor = sb.tile([P, PACK], F32)
+        note_raw = [sb.tile([P, PACK, w], F32, name=f"note_raw{c0}") for c0, w, share in NOTE_CHUNKS]
+        val_pool = [sb.tile([P, T], F32, name=f"val_pool{r}", tag=f"val_pool{r}", align_bytes=64) for r in range(PACK)]
+        held_pool = [sb.tile([P, M], F32, name=f"held_pool{r}", tag=f"held_pool{r}", align_bytes=64) for r in range(PACK)]
+
+        nc.gpsimd.memset(key_scale_pool[:, : T // 2].bitcast(I32), 0)
+        nc.vector.memset(key_scale_pool[:, T // 2 :].bitcast(I32), 0)
+        nc.sync.dma_start(idx[:], offs)
+        nc.sync.dma_start(gain_cols[:], hgain[0:1, :].rearrange("o (p c) -> (o p) c", p=P))
+        nc.sync.dma_start(idx4[:], offs4)
+        nc.sync.dma_start(idx3[:], offs3)
+        nc.sync.dma_start(idx2[:], offs2)
+        nc.sync.dma_start(key_pool[:].bitcast(I32), keys_words[0].bitcast(I32))
+        for q in range(4):
+            nc.sync.dma_start(
+                key_scale_pool[32 * q : 32 * q + 4, :].bitcast(I32), keys_scales[0, 4 * q : 4 * q + 4, :].bitcast(I32)
+            )
+        nc.sync.dma_start(row_factor[:], rowf.rearrange("(p r) o -> p (r o)", r=PACK))
+        notes_v = notes.rearrange("(p t) u -> p t u", t=PACK)
+        for h, (c0, w, share) in enumerate(NOTE_CHUNKS):
+            nc.sync.dma_start(note_raw[h][:], notes_v[:, :, c0 : c0 + w])
+        vals_v = vals.rearrange("(p r) t -> p r t", r=PACK)
+        held_v = held.rearrange("(p r) m -> p r m", r=PACK)
+        for r in range(PACK):
+            nc.sync.dma_start(val_pool[r][:], vals_v[:, r, :])
+        for r in range(PACK):
+            nc.sync.dma_start(held_pool[r][:], held_v[:, r, :])
+
+        ident = sb.tile([P, P], F32)
+        make_identity(nc, ident[:])
+
+        gain_pool = sb.tile([P, M], F32)
+        gain_pool_v = gain_pool[:].rearrange("p (k c) -> p k c", c=M // P)
+        for b in range(2):
+            spread = bank(4 + b, [P, 4, P], "spread")
+            for c in range(4):
+                col = gain_cols[:, 4 * b + c : 4 * b + c + 1]
+                nc.tensor.transpose(spread[:, c, :], col.to_broadcast([P, P]), ident[:])
+            nc.scalar.activation(gain_pool_v[:, :, 4 * b : 4 * b + 4], spread[:].rearrange("p c k -> p k c"), COPY)
+        gain = sb.tile([P, J], F32)
+        nc.scalar.activation(gain[:], gain_pool[:].indirect(idx4[:]), COPY)
+
+        key_listed = sb.tile([P, I], U16, align_bytes=64)
+        key_words = sb.tile([P, I], U16, align_bytes=64)
+        key_scales = sb.tile([P, I], U8, align_bytes=64)
+        nc.vector.tensor_copy(key_listed[:], key_pool[:].indirect(idx[:]))
+        nc.vector.tensor_copy(
+            key_scales[:].rearrange("p (r s) -> p s r", r=PACK), key_scale_pool[:].indirect(idx[:])
+        )
+        nc.vector.tensor_copy(
+            key_words[:].rearrange("p (r s) -> p r s", r=PACK), key_listed[:].rearrange("p (s r) -> p r s", r=PACK)
+        )
+
+        note_bf = [sb.tile([P, w, PACK], BF16, name=f"note_bf{c0}", align_bytes=64) for c0, w, share in NOTE_CHUNKS]
+        note_codes = [sb.tile([P, w], U32, name=f"note_codes{c0}", align_bytes=64) for c0, w, share in NOTE_CHUNKS]
+        note_scales = [sb.tile([P, w], U8, name=f"note_scales{c0}", align_bytes=64) for c0, w, share in NOTE_CHUNKS]
+        g1 = tiles("g1", PACK, [P, U], F32)
+        g1_ps = [[bank(PACK * h + r, [P, BANK], "g1_ps") for r in range(PACK)] for h in range(U // BANK)]
+
+        def copy_out(copy, h, r):
+            copy(out=g1[r][:, h * BANK : (h + 1) * BANK], in_=g1_ps[h][r][:])
+
+        for h, (c0, w, share) in enumerate(NOTE_CHUNKS):
+            interleave(nc.scalar.copy, note_bf[h][:, :share, :], note_raw[h][:, :, :share])
+            if share < w:
+                interleave(nc.vector.tensor_copy, note_bf[h][:, share:, :], note_raw[h][:, :, share:])
+            nc.vector.quantize_mx(
+                out=note_codes[h][:].bitcast(FP8X4),
+                scales=note_scales[h][:],
+                in_=note_bf[h][:].rearrange("p c t -> p (c t)"),
+            )
+            for r in range(PACK):
+                cols = slice(r * P, (r + 1) * P)
+                nc.tensor.matmul_mx(
+                    out=g1_ps[c0 // BANK][r][:, c0 % BANK : c0 % BANK + w],
+                    lhsT=key_words[:, cols].bitcast(FP4X4),
+                    lhsT_scale=key_scales[:, cols],
+                    rhs=note_codes[h][:].bitcast(FP8X4),
+                    rhs_scale=note_scales[h][:],
+                    start=True,
+                    stop=True,
+                )
+
+        val_listed = tiles("val_listed", PACK, [P, I], BF16)
+        val_bf_tags = ["val_bf0", "val_pool2", "val_pool3", "held_pool0"]
+        val_bf = {}
+        val_codes = tiles("val_codes", PACK, [P, P], U32)
+        val_scales = tiles("val_scales", PACK, [P, P], U8)
+
+        def gather_vals(r):
+            window = val_pool[r][:].indirect(idx[:])
+            if r == 0:
+                nc.vector.tensor_copy(val_listed[r][:], window)
+            else:
+                nc.scalar.activation(val_listed[r][:], window, COPY)
+
+        def turn_vals(r):
+            pairs = val_listed[r][:].bitcast(F32)
+            turned = bank(r, [P, 2, P], "turned")
+            val_bf[r] = sb.tile([P, P, PACK], BF16, name=f"val_bf{r}", tag=val_bf_tags[r], align_bytes=64)
+            for u in range(2):
+                nc.tensor.transpose(turned[:, u, :], pairs[:, u : I // 2 : 2], ident[:])
+            copy = nc.vector.tensor_copy if r == 0 else nc.scalar.copy
+            copy(
+                out=val_bf[r][:].rearrange("p e t -> p (e t)").bitcast(F32).rearrange("p (e u) -> p e u", u=2),
+                in_=turned[:].rearrange("p u e -> p e u"),
+            )
+
+        def quantize_vals(r):
+            nc.vector.quantize_mx(
+                out=val_codes[r][:].bitcast(FP8X4),
+                scales=val_scales[r][:],
+                in_=val_bf[r][:].rearrange("p e t -> p (e t)"),
+            )
+
+        minus = tiles("minus", PACK, [P, J], F32)
+        g9 = tiles("g9", PACK, [P, J], F32)
+        gr_bf = sb.tile([P, J, PACK], BF16, align_bytes=64)
+        gr_codes = sb.tile([P, J], U32, align_bytes=64)
+        gr_scales = sb.tile([P, J], U8, align_bytes=64)
+
+        def look_up_minus(r):
+            nc.scalar.activation(minus[r][:], g1[r][:].indirect(idx3[:]), COPY)
+
+        def look_up_plus(r):
+            nc.vector.tensor_tensor(g9[r][:], g1[r][:].indirect(idx2[:]), minus[r][:], ALU.subtract)
+
+        def weigh(r):
+            nc.vector.tensor_scalar(
+                out=gr_bf[:, :, r], in0=g9[r][:], scalar1=0.0, scalar2=row_factor[:, r : r + 1], op0=ALU.max, op1=ALU.mult
+            )
+
+        copy_out(nc.vector.tensor_copy, 0, 0)
+        for r in range(1, PACK):
+            copy_out(nc.scalar.copy, 0, r)
+        for r in range(PACK - 1):
+            copy_out(nc.vector.tensor_copy, 1, r)
+        look_up_minus(0)
+        copy_out(nc.scalar.copy, 1, PACK - 1)
+        for r in range(1, PACK):
+            look_up_minus(r)
+        gather_vals(0)
+        look_up_plus(0)
+        look_up_plus(1)
+        weigh(0)
+        turn_vals(0)
+        look_up_plus(2)
+        weigh(1)
+        look_up_plus(3)
+        weigh(2)
+        quantize_vals(0)
+        weigh(3)
+        nc.vector.quantize_mx(
+            out=gr_codes[:].bitcast(FP8X4), scales=gr_scales[:], in_=gr_bf[:].rearrange("p j t -> p (j t)")
+        )
+
+        gained = tiles("gained", PACK, [P, J], F32)
+        held_listed = tiles("held_listed", PACK - 1, [P, J], F32)
+        y = sb.tile([P, PACK, J], F32)
+        out_v = out_0.rearrange("(p r) j -> p r j", r=PACK)
+
+        def second_product(r):
+            o = bank(PACK + r, [P, J], "o")
+            nc.tensor.matmul_mx(
+                out=o[:],
+                lhsT=val_codes[r][:].bitcast(FP8X4),
+                lhsT_scale=val_scales[r][:],
+                rhs=gr_codes[:].bitcast(FP8X4),
+                rhs_scale=gr_scales[:],
+                start=True,
+                stop=True,
+            )
+            nc.vector.tensor_tensor(gained[r][:], o[:], gain[:], ALU.mult)
+
+        def gather_held(r):
+            nc.scalar.activation(held_listed[r][:], held_pool[r][:].indirect(idx4[:]), COPY)
+
+        def add_held(r):
+            nc.vector.tensor_tensor(y[:, r, :], gained[r][:], held_listed[r][:], ALU.add)
+
+        last = PACK - 1
+        second_product(0)
+        gather_vals(1)
+        gather_vals(2)
+        turn_vals(1)
+        quantize_vals(1)
+        second_product(1)
+        gather_vals(3)
+        turn_vals(2)
+        quantize_vals(2)
+        second_product(2)
+        gather_held(0)
+        turn_vals(3)
+        add_held(0)
+        quantize_vals(3)
+        second_product(3)
+        for r in range(1, last):
+            gather_held(r)
+            add_held(r)
+        nc.sync.dma_start(out_v[:, :last, :], y[:, :last, :])
+        nc.vector.tensor_tensor(y[:, last, :], held_pool[last][:].indirect(idx4[:]), gained[last][:], ALU.add)
+        nc.sync.dma_start(out_v[:, last, :], y[:, last, :])
+
+        y_bf = sb.tile([P, J, PACK], BF16, align_bytes=64)
+        y_codes = sb.tile([P, J], U32, align_bytes=64)
+        y_scales = sb.tile([P, J], U8, align_bytes=64)
+        interleave(nc.scalar.copy, y_bf[:, :Y_SHARE, :], y[:, :, :Y_SHARE])
+        interleave(nc.vector.tensor_copy, y_bf[:, Y_SHARE:, :], y[:, :, Y_SHARE:])
+        nc.vector.quantize_mx(
+            out=y_codes[:].bitcast(FP8X4), scales=y_scales[:], in_=y_bf[:].rearrange("p j t -> p (j t)")
+        )
+        nc.sync.dma_start(out_1[0].rearrange("p c t -> p (c t)").bitcast(I32), y_codes[:].bitcast(I32))
+        for q in range(4):
+            queue = nc.scalar if q < 2 else nc.sync
+            queue.dma_start(out_2[0, 4 * q : 4 * q + 4, :].bitcast(I32), y_scales[32 * q : 32 * q + 4, :].bitcast(I32))

@@ -22,7 +22,7 @@ P = 128
 PACK = 4
 BANK = 512
 Y_SHARE = 80
-NOTE_CHUNKS = ((0, 512, 256), (512, 256, 256), (768, 256, 128))
+NOTE_CHUNKS = ((0, 512, 256), (512, 256, 256), (768, 256, 0))
 
 
 def interleave(copy, dst, src):
@@ -58,20 +58,20 @@ def tile_attend_tab_looked_merge_pl_kernel(
 
         nc.gpsimd.memset(key_scale_pool[:, : T // 2].bitcast(I32), 0)
         nc.vector.memset(key_scale_pool[:, T // 2 :].bitcast(I32), 0)
+        notes_v = notes.rearrange("(p t) u -> p t u", t=PACK)
         nc.sync.dma_start(idx[:], offs)
         nc.sync.dma_start(gain_cols[:], hgain[0:1, :].rearrange("o (p c) -> (o p) c", p=P))
         nc.sync.dma_start(idx4[:], offs4)
-        nc.sync.dma_start(idx3[:], offs3)
-        nc.sync.dma_start(idx2[:], offs2)
         nc.sync.dma_start(key_pool[:].bitcast(I32), keys_words[0].bitcast(I32))
         for q in range(4):
             nc.sync.dma_start(
                 key_scale_pool[32 * q : 32 * q + 4, :].bitcast(I32), keys_scales[0, 4 * q : 4 * q + 4, :].bitcast(I32)
             )
+        nc.sync.dma_start(idx3[:], offs3)
+        nc.sync.dma_start(idx2[:], offs2)
+        for n, (c0, w, share) in enumerate(NOTE_CHUNKS):
+            nc.sync.dma_start(note_raw[n][:], notes_v[:, :, c0 : c0 + w])
         nc.sync.dma_start(row_factor[:], rowf.rearrange("(p r) o -> p (r o)", r=PACK))
-        notes_v = notes.rearrange("(p t) u -> p t u", t=PACK)
-        for h, (c0, w, share) in enumerate(NOTE_CHUNKS):
-            nc.sync.dma_start(note_raw[h][:], notes_v[:, :, c0 : c0 + w])
         vals_v = vals.rearrange("(p r) t -> p r t", r=PACK)
         held_v = held.rearrange("(p r) m -> p r m", r=PACK)
         for r in range(PACK):
@@ -104,48 +104,49 @@ def tile_attend_tab_looked_merge_pl_kernel(
             key_words[:].rearrange("p (r s) -> p r s", r=PACK), key_listed[:].rearrange("p (s r) -> p r s", r=PACK)
         )
 
-        note_bf = [sb.tile([P, w, PACK], BF16, name=f"note_bf{c0}", align_bytes=64) for c0, w, share in NOTE_CHUNKS]
-        note_codes = [sb.tile([P, w], U32, name=f"note_codes{c0}", align_bytes=64) for c0, w, share in NOTE_CHUNKS]
-        note_scales = [sb.tile([P, w], U8, name=f"note_scales{c0}", align_bytes=64) for c0, w, share in NOTE_CHUNKS]
+        note_bf = tiles("note_bf", U // BANK, [P, BANK, PACK], BF16)
+        note_codes = tiles("note_codes", U // BANK, [P, BANK], U32)
+        note_scales = tiles("note_scales", U // BANK, [P, BANK], U8)
         g1 = tiles("g1", PACK, [P, U], F32)
         g1_ps = [[bank(PACK * h + r, [P, BANK], "g1_ps") for r in range(PACK)] for h in range(U // BANK)]
 
         def copy_out(copy, h, r):
             copy(out=g1[r][:, h * BANK : (h + 1) * BANK], in_=g1_ps[h][r][:])
 
-        for h, (c0, w, share) in enumerate(NOTE_CHUNKS):
-            interleave(nc.scalar.copy, note_bf[h][:, :share, :], note_raw[h][:, :, :share])
+        for n, (c0, w, share) in enumerate(NOTE_CHUNKS):
+            h, lo = divmod(c0, BANK)
+            if share:
+                interleave(nc.scalar.copy, note_bf[h][:, lo : lo + share, :], note_raw[n][:, :, :share])
             if share < w:
-                interleave(nc.vector.tensor_copy, note_bf[h][:, share:, :], note_raw[h][:, :, share:])
+                interleave(nc.vector.tensor_copy, note_bf[h][:, lo + share : lo + w, :], note_raw[n][:, :, share:])
+            if lo + w < BANK:
+                continue
             nc.vector.quantize_mx(
                 out=note_codes[h][:].bitcast(FP8X4),
                 scales=note_scales[h][:],
                 in_=note_bf[h][:].rearrange("p c t -> p (c t)"),
             )
-            for r in range(PACK):
-                cols = slice(r * P, (r + 1) * P)
-                nc.tensor.matmul_mx(
-                    out=g1_ps[c0 // BANK][r][:, c0 % BANK : c0 % BANK + w],
-                    lhsT=key_words[:, cols].bitcast(FP4X4),
-                    lhsT_scale=key_scales[:, cols],
-                    rhs=note_codes[h][:].bitcast(FP8X4),
-                    rhs_scale=note_scales[h][:],
-                    start=True,
-                    stop=True,
-                )
+
+        def first_product(h, r):
+            cols = slice(r * P, (r + 1) * P)
+            nc.tensor.matmul_mx(
+                out=g1_ps[h][r][:],
+                lhsT=key_words[:, cols].bitcast(FP4X4),
+                lhsT_scale=key_scales[:, cols],
+                rhs=note_codes[h][:].bitcast(FP8X4),
+                rhs_scale=note_scales[h][:],
+                start=True,
+                stop=True,
+            )
 
         val_listed = tiles("val_listed", PACK, [P, I], BF16)
-        val_bf_tags = ["val_bf0", "val_pool2", "val_pool3", "held_pool0"]
+        val_bf_tags = ["val_bf0", "val_pool2", "val_pool3", "val_bf3"]
         val_bf = {}
         val_codes = tiles("val_codes", PACK, [P, P], U32)
         val_scales = tiles("val_scales", PACK, [P, P], U8)
 
         def gather_vals(r):
-            window = val_pool[r][:].indirect(idx[:])
-            if r == 0:
-                nc.vector.tensor_copy(val_listed[r][:], window)
-            else:
-                nc.scalar.activation(val_listed[r][:], window, COPY)
+            nc.scalar.activation(val_listed[r][:], val_pool[r][:].indirect(idx[:]), COPY)
 
         def turn_vals(r):
             pairs = val_listed[r][:].bitcast(F32)
@@ -153,8 +154,7 @@ def tile_attend_tab_looked_merge_pl_kernel(
             val_bf[r] = sb.tile([P, P, PACK], BF16, name=f"val_bf{r}", tag=val_bf_tags[r], align_bytes=64)
             for u in range(2):
                 nc.tensor.transpose(turned[:, u, :], pairs[:, u : I // 2 : 2], ident[:])
-            copy = nc.vector.tensor_copy if r == 0 else nc.scalar.copy
-            copy(
+            nc.scalar.copy(
                 out=val_bf[r][:].rearrange("p e t -> p (e t)").bitcast(F32).rearrange("p (e u) -> p e u", u=2),
                 in_=turned[:].rearrange("p u e -> p e u"),
             )
@@ -183,32 +183,27 @@ def tile_attend_tab_looked_merge_pl_kernel(
                 out=gr_bf[:, :, r], in0=g9[r][:], scalar1=0.0, scalar2=row_factor[:, r : r + 1], op0=ALU.max, op1=ALU.mult
             )
 
-        copy_out(nc.vector.tensor_copy, 0, 0)
-        for r in range(1, PACK):
-            copy_out(nc.scalar.copy, 0, r)
-        for r in range(PACK - 1):
+        for r in range(PACK):
+            first_product(0, r)
+            first_product(1, r)
+            copy_out(nc.scalar.copy if r < PACK - 1 else nc.vector.tensor_copy, 0, r)
             copy_out(nc.vector.tensor_copy, 1, r)
-        look_up_minus(0)
-        copy_out(nc.scalar.copy, 1, PACK - 1)
-        for r in range(1, PACK):
+        for r in range(PACK):
             look_up_minus(r)
-        gather_vals(0)
         look_up_plus(0)
-        look_up_plus(1)
-        weigh(0)
+        for r in range(1, PACK):
+            look_up_plus(r)
+            weigh(r - 1)
+        gather_vals(0)
         turn_vals(0)
-        look_up_plus(2)
-        weigh(1)
-        look_up_plus(3)
-        weigh(2)
         quantize_vals(0)
-        weigh(3)
+        weigh(PACK - 1)
         nc.vector.quantize_mx(
             out=gr_codes[:].bitcast(FP8X4), scales=gr_scales[:], in_=gr_bf[:].rearrange("p j t -> p (j t)")
         )
 
-        gained = tiles("gained", PACK, [P, J], F32)
-        held_listed = tiles("held_listed", PACK - 1, [P, J], F32)
+        gained = {}
+        held_listed = {r: sb.tile([P, J], F32, name=f"held_listed{r}") for r in range(1, PACK)}
         y = sb.tile([P, PACK, J], F32)
         out_v = out_0.rearrange("(p r) j -> p r j", r=PACK)
 
@@ -223,6 +218,8 @@ def tile_attend_tab_looked_merge_pl_kernel(
                 start=True,
                 stop=True,
             )
+            tag = "held_pool0" if r == 1 else f"gained{r}"
+            gained[r] = sb.tile([P, J], F32, name=f"gained{r}", tag=tag, align_bytes=64)
             nc.vector.tensor_tensor(gained[r][:], o[:], gain[:], ALU.mult)
 
         def gather_held(r):
@@ -237,21 +234,21 @@ def tile_attend_tab_looked_merge_pl_kernel(
         gather_vals(2)
         turn_vals(1)
         quantize_vals(1)
+        nc.vector.tensor_tensor(y[:, 0, :], held_pool[0][:].indirect(idx4[:]), gained[0][:], ALU.add)
         second_product(1)
         gather_vals(3)
         turn_vals(2)
-        quantize_vals(2)
-        second_product(2)
-        gather_held(0)
         turn_vals(3)
-        add_held(0)
+        quantize_vals(2)
         quantize_vals(3)
+        second_product(2)
         second_product(3)
         for r in range(1, last):
             gather_held(r)
             add_held(r)
         nc.sync.dma_start(out_v[:, :last, :], y[:, :last, :])
-        nc.vector.tensor_tensor(y[:, last, :], held_pool[last][:].indirect(idx4[:]), gained[last][:], ALU.add)
+        gather_held(last)
+        add_held(last)
         nc.sync.dma_start(out_v[:, last, :], y[:, last, :])
 
         y_bf = sb.tile([P, J, PACK], BF16, align_bytes=64)

from contextlib import ExitStack

import concourse.mybir as mybir
from concourse.masks import make_identity

D, T, I, J, U, E, M = 512, 2048, 512, 256, 1024, 512, 1024
FLOPS = 2 * D * I * U + 2 * I * E * J
BYTES = 9631744

F32 = mybir.dt.float32
BF16 = mybir.dt.bfloat16
I32 = mybir.dt.int32
U32 = mybir.dt.uint32
U16 = mybir.dt.uint16
U8 = mybir.dt.uint8
FP8X4 = mybir.dt.float8_e4m3fn_x4
FP4X4 = mybir.dt.float4_e2m1fn_x4
ALU = mybir.AluOpType
COPY = mybir.ActivationFunctionType.Copy

P = 128
PACK = 4
BANK = 512
Y_SHARE = 80
NOTE_CHUNKS = ((0, 512, 256), (512, 256, 256), (768, 256, 0))


def interleave(copy, dst, src):
    copy(out=dst.rearrange("p (c i) t -> p c t i", i=4), in_=src.rearrange("p t (c i) -> p c t i", i=4))


def tile_attend_tab_looked_merge_pl_kernel(
    tc, keys_words, keys_scales, notes, rowf, vals, held, hgain, offs, offs2, offs3, offs4, out_0, out_1, out_2
):
    nc = tc.nc
    with ExitStack() as ctx:
        lists = ctx.enter_context(tc.tile_pool(name="lists", bufs=1))
        sb = ctx.enter_context(tc.tile_pool(name="sb", bufs=1))
        ps = ctx.enter_context(tc.psum_pool(name="ps", bufs=1))

        def bank(n, shape, name):
            return ps.tile(shape, F32, name=name, tag=f"bank{n}")

        def tiles(name, count, shape, dtype):
            return [sb.tile(shape, dtype, name=f"{name}{n}", align_bytes=64) for n in range(count)]

        idx = lists.tile([P, I // 16], U16)
        idx2 = lists.tile([P, J // 16], U16)
        idx3 = lists.tile([P, J // 16], U16)
        idx4 = lists.tile([P, J // 16], U16)
        key_pool = sb.tile([P, T], U16, align_bytes=64)
        key_scale_pool = sb.tile([P, T], U8, align_bytes=64)
        gain_cols = sb.tile([P, M // P], F32)
        row_factor = sb.tile([P, PACK], F32)
        note_raw = [sb.tile([P, PACK, w], F32, name=f"note_raw{c0}") for c0, w, share in NOTE_CHUNKS]
        val_pool = [sb.tile([P, T], F32, name=f"val_pool{r}", tag=f"val_pool{r}", align_bytes=64) for r in range(PACK)]
        held_pool = [sb.tile([P, M], F32, name=f"held_pool{r}", tag=f"held_pool{r}", align_bytes=64) for r in range(PACK)]

        nc.gpsimd.memset(key_scale_pool[:, : T // 2].bitcast(I32), 0)
        nc.vector.memset(key_scale_pool[:, T // 2 :].bitcast(I32), 0)
        notes_v = notes.rearrange("(p t) u -> p t u", t=PACK)
        nc.sync.dma_start(idx[:], offs)
        nc.sync.dma_start(gain_cols[:], hgain[0:1, :].rearrange("o (p c) -> (o p) c", p=P))
        nc.sync.dma_start(idx4[:], offs4)
        nc.sync.dma_start(key_pool[:].bitcast(I32), keys_words[0].bitcast(I32))
        for q in range(4):
            nc.sync.dma_start(
                key_scale_pool[32 * q : 32 * q + 4, :].bitcast(I32), keys_scales[0, 4 * q : 4 * q + 4, :].bitcast(I32)
            )
        nc.sync.dma_start(idx3[:], offs3)
        nc.sync.dma_start(idx2[:], offs2)
        for n, (c0, w, share) in enumerate(NOTE_CHUNKS):
            nc.sync.dma_start(note_raw[n][:], notes_v[:, :, c0 : c0 + w])
        nc.sync.dma_start(row_factor[:], rowf.rearrange("(p r) o -> p (r o)", r=PACK))
        vals_v = vals.rearrange("(p r) t -> p r t", r=PACK)
        held_v = held.rearrange("(p r) m -> p r m", r=PACK)
        for r in range(PACK):
            nc.sync.dma_start(val_pool[r][:], vals_v[:, r, :])
        for r in range(PACK):
            nc.sync.dma_start(held_pool[r][:], held_v[:, r, :])

        ident = sb.tile([P, P], F32)
        make_identity(nc, ident[:])

        gain_pool = sb.tile([P, M], F32)
        gain_pool_v = gain_pool[:].rearrange("p (k c) -> p k c", c=M // P)
        for b in range(2):
            spread = bank(4 + b, [P, 4, P], "spread")
            for c in range(4):
                col = gain_cols[:, 4 * b + c : 4 * b + c + 1]
                nc.tensor.transpose(spread[:, c, :], col.to_broadcast([P, P]), ident[:])
            nc.scalar.activation(gain_pool_v[:, :, 4 * b : 4 * b + 4], spread[:].rearrange("p c k -> p k c"), COPY)
        gain = sb.tile([P, J], F32)
        nc.scalar.activation(gain[:], gain_pool[:].indirect(idx4[:]), COPY)

        key_listed = sb.tile([P, I], U16, align_bytes=64)
        key_words = sb.tile([P, I], U16, align_bytes=64)
        key_scales = sb.tile([P, I], U8, align_bytes=64)
        nc.vector.tensor_copy(key_listed[:], key_pool[:].indirect(idx[:]))
        nc.vector.tensor_copy(
            key_scales[:].rearrange("p (r s) -> p s r", r=PACK), key_scale_pool[:].indirect(idx[:])
        )
        nc.vector.tensor_copy(
            key_words[:].rearrange("p (r s) -> p r s", r=PACK), key_listed[:].rearrange("p (s r) -> p r s", r=PACK)
        )

        note_bf = tiles("note_bf", U // BANK, [P, BANK, PACK], BF16)
        note_codes = tiles("note_codes", U // BANK, [P, BANK], U32)
        note_scales = tiles("note_scales", U // BANK, [P, BANK], U8)
        g1 = tiles("g1", PACK, [P, U], F32)
        g1_ps = [[bank(PACK * h + r, [P, BANK], "g1_ps") for r in range(PACK)] for h in range(U // BANK)]

        def copy_out(copy, h, r):
            copy(out=g1[r][:, h * BANK : (h + 1) * BANK], in_=g1_ps[h][r][:])

        for n, (c0, w, share) in enumerate(NOTE_CHUNKS):
            h, lo = divmod(c0, BANK)
            if share:
                interleave(nc.scalar.copy, note_bf[h][:, lo : lo + share, :], note_raw[n][:, :, :share])
            if share < w:
                interleave(nc.vector.tensor_copy, note_bf[h][:, lo + share : lo + w, :], note_raw[n][:, :, share:])
            if lo + w < BANK:
                continue
            nc.vector.quantize_mx(
                out=note_codes[h][:].bitcast(FP8X4),
                scales=note_scales[h][:],
                in_=note_bf[h][:].rearrange("p c t -> p (c t)"),
            )

        def first_product(h, r):
            cols = slice(r * P, (r + 1) * P)
            nc.tensor.matmul_mx(
                out=g1_ps[h][r][:],
                lhsT=key_words[:, cols].bitcast(FP4X4),
                lhsT_scale=key_scales[:, cols],
                rhs=note_codes[h][:].bitcast(FP8X4),
                rhs_scale=note_scales[h][:],
                start=True,
                stop=True,
            )

        val_listed = tiles("val_listed", PACK, [P, I], BF16)
        val_bf_tags = ["val_bf0", "val_pool2", "val_pool3", "val_bf3"]
        val_bf = {}
        val_codes = tiles("val_codes", PACK, [P, P], U32)
        val_scales = tiles("val_scales", PACK, [P, P], U8)

        def gather_vals(r):
            nc.scalar.activation(val_listed[r][:], val_pool[r][:].indirect(idx[:]), COPY)

        def turn_vals(r):
            pairs = val_listed[r][:].bitcast(F32)
            turned = bank(r, [P, 2, P], "turned")
            val_bf[r] = sb.tile([P, P, PACK], BF16, name=f"val_bf{r}", tag=val_bf_tags[r], align_bytes=64)
            for u in range(2):
                nc.tensor.transpose(turned[:, u, :], pairs[:, u : I // 2 : 2], ident[:])
            nc.scalar.copy(
                out=val_bf[r][:].rearrange("p e t -> p (e t)").bitcast(F32).rearrange("p (e u) -> p e u", u=2),
                in_=turned[:].rearrange("p u e -> p e u"),
            )

        def quantize_vals(r):
            nc.vector.quantize_mx(
                out=val_codes[r][:].bitcast(FP8X4),
                scales=val_scales[r][:],
                in_=val_bf[r][:].rearrange("p e t -> p (e t)"),
            )

        minus = tiles("minus", PACK, [P, J], F32)
        g9 = tiles("g9", PACK, [P, J], F32)
        gr_bf = sb.tile([P, J, PACK], BF16, align_bytes=64)
        gr_codes = sb.tile([P, J], U32, align_bytes=64)
        gr_scales = sb.tile([P, J], U8, align_bytes=64)

        def look_up_minus(r):
            nc.scalar.activation(minus[r][:], g1[r][:].indirect(idx3[:]), COPY)

        def look_up_plus(r):
            nc.vector.tensor_tensor(g9[r][:], g1[r][:].indirect(idx2[:]), minus[r][:], ALU.subtract)

        def weigh(r):
            nc.vector.tensor_scalar(
                out=gr_bf[:, :, r], in0=g9[r][:], scalar1=0.0, scalar2=row_factor[:, r : r + 1], op0=ALU.max, op1=ALU.mult
            )

        for r in range(PACK):
            first_product(0, r)
            first_product(1, r)
            copy_out(nc.scalar.copy if r < PACK - 1 else nc.vector.tensor_copy, 0, r)
            copy_out(nc.vector.tensor_copy, 1, r)
        for r in range(PACK):
            look_up_minus(r)
        look_up_plus(0)
        for r in range(1, PACK):
            look_up_plus(r)
            weigh(r - 1)
        gather_vals(0)
        turn_vals(0)
        quantize_vals(0)
        weigh(PACK - 1)
        nc.vector.quantize_mx(
            out=gr_codes[:].bitcast(FP8X4), scales=gr_scales[:], in_=gr_bf[:].rearrange("p j t -> p (j t)")
        )

        gained = {}
        held_listed = {r: sb.tile([P, J], F32, name=f"held_listed{r}") for r in range(1, PACK)}
        y = sb.tile([P, PACK, J], F32)
        out_v = out_0.rearrange("(p r) j -> p r j", r=PACK)

        def second_product(r):
            o = bank(PACK + r, [P, J], "o")
            nc.tensor.matmul_mx(
                out=o[:],
                lhsT=val_codes[r][:].bitcast(FP8X4),
                lhsT_scale=val_scales[r][:],
                rhs=gr_codes[:].bitcast(FP8X4),
                rhs_scale=gr_scales[:],
                start=True,
                stop=True,
            )
            tag = "held_pool0" if r == 1 else f"gained{r}"
            gained[r] = sb.tile([P, J], F32, name=f"gained{r}", tag=tag, align_bytes=64)
            nc.vector.tensor_tensor(gained[r][:], o[:], gain[:], ALU.mult)

        def gather_held(r):
            nc.scalar.activation(held_listed[r][:], held_pool[r][:].indirect(idx4[:]), COPY)

        def add_held(r):
            nc.vector.tensor_tensor(y[:, r, :], gained[r][:], held_listed[r][:], ALU.add)

        last = PACK - 1
        second_product(0)
        gather_vals(1)
        gather_vals(2)
        turn_vals(1)
        quantize_vals(1)
        nc.vector.tensor_tensor(y[:, 0, :], held_pool[0][:].indirect(idx4[:]), gained[0][:], ALU.add)
        second_product(1)
        gather_vals(3)
        turn_vals(2)
        turn_vals(3)
        quantize_vals(2)
        quantize_vals(3)
        second_product(2)
        second_product(3)
        for r in range(1, last):
            gather_held(r)
            add_held(r)
        nc.sync.dma_start(out_v[:, :last, :], y[:, :last, :])
        gather_held(last)
        add_held(last)
        nc.sync.dma_start(out_v[:, last, :], y[:, last, :])

        y_bf = sb.tile([P, J, PACK], BF16, align_bytes=64)
        y_codes = sb.tile([P, J], U32, align_bytes=64)
        y_scales = sb.tile([P, J], U8, align_bytes=64)
        interleave(nc.scalar.copy, y_bf[:, :Y_SHARE, :], y[:, :, :Y_SHARE])
        interleave(nc.vector.tensor_copy, y_bf[:, Y_SHARE:, :], y[:, :, Y_SHARE:])
        nc.vector.quantize_mx(
            out=y_codes[:].bitcast(FP8X4), scales=y_scales[:], in_=y_bf[:].rearrange("p j t -> p (j t)")
        )
        nc.sync.dma_start(out_1[0].rearrange("p c t -> p (c t)").bitcast(I32), y_codes[:].bitcast(I32))
        for q in range(4):
            queue = nc.scalar if q < 2 else nc.sync
            queue.dma_start(out_2[0, 4 * q : 4 * q + 4, :].bitcast(I32), y_scales[32 * q : 32 * q + 4, :].bitcast(I32))
